import numpy as np
import ml_dtypes


def mxq(x, axis, fmt="e4m3"):
    dtype, down = {"e4m3": (ml_dtypes.float8_e4m3fn, 7), "e5m2": (ml_dtypes.float8_e5m2, 14)}[fmt]
    v = np.moveaxis(np.asarray(x, np.float32).astype(ml_dtypes.bfloat16).astype(np.float64), axis, -1)
    blocks = v.reshape(v.shape[:-1] + (-1, 32))
    amax = np.abs(blocks).max(-1, keepdims=True)
    byte = np.maximum(np.where(amax > 0, np.frexp(amax)[1] - 1 + 127, 0) - down, 1)
    scale = np.exp2(byte - 127.0)
    codes = (blocks / scale).astype(np.float32).astype(dtype).astype(np.float64)
    return np.moveaxis((codes * scale).reshape(v.shape), -1, axis)


WIDE = False


def mx_kscale(k):
    if not WIDE:
        return np.ones(k)
    levels = np.array([10, -10, 5, -5, 0])
    if k % 512:
        return np.exp2(np.random.permutation(np.resize(levels, k // 32))).repeat(32)
    a = np.empty((k // 512, 16))
    for p in range(k // 512):
        a[p, :8] = np.random.permutation(np.resize(levels, 8))
        for g in range(8):
            far = levels[np.abs(levels - a[p, g]) >= 10]
            a[p, g + 8] = far[np.random.randint(len(far))]
    return np.exp2(a.ravel()).repeat(32)


def f64(x):
    return np.asarray(x).astype(np.float64)


def striped(idx):
    return np.tile(idx.reshape(-1, 16).T, (8, 1)).astype(np.uint16)


def unstriped(offs):
    return offs[:16].T.reshape(-1).astype(np.int64)


def pack_weight(w):
    k, n = w.shape
    w = f64(np.asarray(w, np.float32).astype(ml_dtypes.bfloat16)).reshape(k // 32, 32, n)
    amax = np.abs(w).max(1)
    byte = np.clip(np.where(amax > 0, np.frexp(amax)[1] - 1 + 127 - 7, 1), 1, 254)
    scaled = (w * np.exp2(127.0 - byte)[:, None, :]).reshape(k, n).astype(np.float32)
    words = np.ascontiguousarray(scaled.reshape(k // 512, 128, 4, n).transpose(0, 1, 3, 2)).astype(ml_dtypes.float8_e4m3fn).view(np.uint8)
    return words, np.ascontiguousarray(byte.astype(np.uint8).reshape(k // 512, 16, n))


def unpack_weight(words, scales):
    g, p, n, _ = words.shape
    vals = np.ascontiguousarray(words).view(ml_dtypes.float8_e4m3fn).astype(np.float64) * np.repeat(np.exp2(scales.astype(np.float64) - 127.0), 8, axis=1)[..., None]
    return vals.transpose(0, 1, 3, 2).reshape(g * 512, n)


def relu(v):
    return np.maximum(v, 0.0)


K, T, S, V = 512, 2048, 512, 256
P = 2 ** 7


def setup_inputs():
    n = np.random.standard_normal
    s = mx_kscale(K)[:, None]
    packed_xT = pack_weight(n((K, T)) * s)
    return {
        "x_words": packed_xT[0],
        "x_scales": packed_xT[1],
        "hT": (n((K, V)) / np.sqrt(K) / s).astype(np.float32),
        "lab": (np.eye(S)[np.random.randint(0, S, V)]).astype(np.float32),
        "lcnt": (np.tile(np.random.uniform(0.0, 6.0, T), (P, 1))).astype(np.float32),
        "lown": (-np.random.uniform(0.0, 3.0, (V, 1))).astype(np.float32),
        "offs": striped(np.random.permutation(T)[:S]),
    }


def reference(x_words, x_scales, hT, lab, lcnt, lown, offs):
    hTq = mxq(f64(hT), 0, "e4m3")
    xq = unpack_weight(x_words, x_scales)[:, unstriped(offs)]
    y = 1.2 * (hTq.T @ xq)
    mit = np.minimum(0.5 * (f64(lcnt)[:1][:, unstriped(offs)]) + f64(lown), 0.05 * (f64(lcnt)[:1][:, unstriped(offs)]))
    ex = np.exp(y - y.max(axis=1, keepdims=True))
    pr = ex / ex.sum(axis=1, keepdims=True)
    pl = pr * f64(lab)
    pt = pl.sum(axis=1, keepdims=True) + 0.0005
    cmp = relu(np.log(pr / pt))
    ys = y + (-1.0 * f64(lab) + 1.0) * (mit + 0.8 * cmp)
    ez = np.exp(ys)
    tz = ez.sum(axis=1, keepdims=True)
    return ys - np.log(tz)

@@ -1,0 +1,167 @@
+import math
+from contextlib import ExitStack
+
+import concourse.mybir as mybir
+from concourse.masks import make_identity
+
+K, T, S, V = 512, 2048, 512, 256
+FLOPS = 2 * K * S * V
+
+F32 = mybir.dt.float32
+BF16 = mybir.dt.bfloat16
+I32 = mybir.dt.int32
+U32 = mybir.dt.uint32
+U16 = mybir.dt.uint16
+U8 = mybir.dt.uint8
+FP8X4 = mybir.dt.float8_e4m3fn_x4
+ALU = mybir.AluOpType
+ACT = mybir.ActivationFunctionType
+
+P = 128
+PACK = 4
+BLOCKS = V // P
+CHUNKS = S // P
+ROW = P - 1
+
+GAIN = 1.2
+KINK = 0.8 * GAIN
+DEG = 16
+LN2 = math.log(2.0)
+BITS_SCALE = LN2 / 2.0**23
+BITS_BIAS = -88.0
+POLY = [0.0] + [(-1.0) ** (n + 1) / n for n in range(1, DEG + 1)]
+STEPS = DEG + 1
+
+
+def tile_picked_yseesw_lp_p_kernel(tc, x_words, x_scales, hT, lab, lcnt, lown, offs, out):
+    nc = tc.nc
+    with ExitStack() as ctx:
+        sb = ctx.enter_context(tc.tile_pool(name="sb", bufs=1))
+        ps = ctx.enter_context(tc.psum_pool(name="ps", bufs=1))
+
+        offsets = sb.tile([P, S // 16], U16, name="offsets")
+        scale_window = sb.tile([P, T], U8, name="scale_window")
+        count_window = sb.tile([P, T], F32, name="count_window")
+        word_window = sb.tile([P, T], I32, name="word_window")
+        own = sb.tile([P, BLOCKS], F32, name="own")
+        h_raw = sb.tile([P, PACK, V], F32, name="h_raw")
+        labels = [sb.tile([P, S], F32, name="labels%d" % b) for b in range(BLOCKS)]
+
+        nc.vector.memset(scale_window[:].bitcast(I32), 0)
+        nc.vector.memset(count_window[0:ROW, 0 : T // 2], 0.0)
+        nc.gpsimd.memset(count_window[0:ROW, T // 2 : T], 0.0)
+        nc.sync.dma_start(offsets[:], offs)
+        nc.sync.dma_start(out=count_window[ROW:P, :], in_=lcnt[0:1, :])
+        for q in range(4):
+            nc.sync.dma_start(out=scale_window[32 * q : 32 * q + 4, :].bitcast(I32), in_=x_scales[0, 4 * q : 4 * q + 4, :].bitcast(I32))
+        with nc.allow_non_contiguous_dma(reason="one value a partition"):
+            nc.sync.dma_start(out=own[:], in_=lown.rearrange("(b p) o -> p (b o)", p=P))
+        nc.sync.dma_start(out=word_window[:], in_=x_words[0].rearrange("p n t -> p (n t)").bitcast(I32))
+        nc.sync.dma_start(out=h_raw[:], in_=hT.rearrange("(p j) c -> p j c", j=PACK))
+        for b in range(BLOCKS):
+            nc.sync.dma_start(out=labels[b][:], in_=lab[b * P : (b + 1) * P, :])
+
+        ident = sb.tile([P, P], F32, name="ident")
+        make_identity(nc, ident[:])
+        one = sb.tile([P, 1], F32, name="one")
+        nc.gpsimd.memset(one[:], 1.0)
+
+        addends = sb.tile([P, 2 * BLOCKS, 24], F32, name="addends")
+        for i in range(DEG):
+            nc.scalar.activation(out=addends[:, :, DEG - 1 - i], in_=one[:].to_broadcast([P, 2 * BLOCKS]), func=ACT.Copy, scale=POLY[i])
+        gains = [1.0 / GAIN, -1.0]
+        factors = [sb.tile([P, STEPS], F32, name="factors%d" % n) for n in range(2 * BLOCKS)]
+        for n in range(2 * BLOCKS):
+            nc.scalar.activation(out=factors[n][:, STEPS - 1 : STEPS], in_=one[:], func=ACT.Copy, scale=gains[n // BLOCKS])
+
+        def scaled_log(n, total, shift):
+            bits = total.bitcast(U32)
+            inverse = sb.tile([P, 1], F32, name="inverse%d" % n)
+            nc.scalar.activation(out=inverse[:], in_=bits, func=ACT.Exp, scale=-BITS_SCALE, bias=-BITS_BIAS)
+            nc.scalar.activation(out=addends[:, n, DEG:STEPS], in_=bits, func=ACT.Identity, scale=gains[n // BLOCKS] * BITS_SCALE, bias=shift)
+            nc.scalar.activation(out=factors[n][:, 0:DEG], in_=inverse[:].to_broadcast([P, DEG]), func=ACT.Copy, scale=total, bias=-1.0)
+            horner = sb.tile([P, STEPS], F32, name="horner%d" % n)
+            nc.vector.tensor_tensor_scan(out=horner[:], data0=factors[n][:], data1=addends[:, n, 0:STEPS], initial=POLY[DEG], op0=ALU.mult, op1=ALU.add)
+            return horner[:, STEPS - 1 : STEPS]
+
+        counts = sb.tile([P, S], F32, name="counts")
+        nc.vector.tensor_copy(out=counts[:], in_=count_window[:].indirect(offsets[:]))
+        x_scale = sb.tile([P, S], U8, name="x_scale", align_bytes=64)
+        nc.vector.tensor_copy(out=x_scale[:], in_=scale_window[:].indirect(offsets[:]))
+        x_codes = sb.tile([P, S], U32, name="x_codes", align_bytes=64)
+        nc.vector.tensor_copy(out=x_codes[:], in_=word_window[:].bitcast(U32).indirect(offsets[:]))
+
+        own_rows = ps.tile([P, V], F32, name="own_rows")
+        for b in range(BLOCKS):
+            nc.tensor.transpose(own_rows[:, b * P : (b + 1) * P], own[:, b : b + 1].to_broadcast([P, P]), ident[:])
+        counts_t = ps.tile([P, CHUNKS, P], F32, name="counts_t")
+        for c in range(CHUNKS):
+            nc.tensor.transpose(counts_t[:, c, :], counts[:, c * P : (c + 1) * P], ident[:])
+        gap_col = sb.tile([P, CHUNKS], F32, name="gap_col")
+        cap_col = sb.tile([P, CHUNKS], F32, name="cap_col")
+        nc.scalar.activation(out=gap_col[:], in_=counts_t[:, :, ROW], func=ACT.Copy, scale=-0.45 / KINK)
+        nc.scalar.activation(out=cap_col[:], in_=counts_t[:, :, ROW], func=ACT.Copy, scale=-0.05 / KINK)
+        neg_mit = [ps.tile([P, S], F32, name="neg_mit%d" % b) for b in range(BLOCKS)]
+        for b in range(BLOCKS):
+            for c in range(CHUNKS):
+                nc.tensor.matmul(neg_mit[b][:, c * P : (c + 1) * P], lhsT=cap_col[:, c : c + 1].to_broadcast([P, P]), rhs=ident[:], is_transpose=True, start=(c == 0), stop=False)
+        for c in range(CHUNKS):
+            short_t = sb.tile([P, V], F32, name="short_t%d" % c)
+            nc.scalar.activation(out=short_t[:], in_=own_rows[:], func=ACT.Relu, scale=-1.0 / KINK, bias=gap_col[:, c : c + 1])
+            for b in range(BLOCKS):
+                nc.tensor.matmul(neg_mit[b][:, c * P : (c + 1) * P], lhsT=short_t[:, b * P : (b + 1) * P], rhs=ident[:], is_transpose=True, start=False, stop=(c == CHUNKS - 1))
+
+        grouped = [sb.tile([P, P, PACK], BF16, name="grouped%d" % b, align_bytes=64) for b in range(BLOCKS)]
+        nc.vector.tensor_copy(out=grouped[0][:], in_=h_raw[:, :, 0:P].rearrange("p j c -> p c j"))
+        nc.scalar.copy(out=grouped[1][:], in_=h_raw[:, :, P : 2 * P].rearrange("p j c -> p c j"))
+        z = []
+        for b in range(BLOCKS):
+            h_codes = sb.tile([P, P], U32, name="h_codes%d" % b, align_bytes=64)
+            h_scale = sb.tile([P, P], U8, name="h_scale%d" % b, align_bytes=64)
+            nc.vector.quantize_mx(out=h_codes[:].bitcast(FP8X4), scales=h_scale[:], in_=grouped[b][:].rearrange("p c j -> p (c j)"))
+            zb = ps.tile([P, S], F32, name="z%d" % b)
+            nc.tensor.matmul_mx(out=zb[:], lhsT=h_codes[:].bitcast(FP8X4), lhsT_scale=h_scale[:], rhs=x_codes[:].bitcast(FP8X4), rhs_scale=x_scale[:], start=True, stop=True)
+            z.append(zb)
+
+        def big(name, b):
+            return sb.tile([P, S], F32, name="%s%d" % (name, b))
+
+        def col(name, b):
+            return sb.tile([P, 1], F32, name="%s%d" % (name, b))
+
+        masked = [big("masked", b) for b in range(BLOCKS)]
+        neg_y = [big("neg_y", b) for b in range(BLOCKS)]
+        ex = [big("ex", b) for b in range(BLOCKS)]
+        weighted = [big("weighted", b) for b in range(BLOCKS)]
+        base = [big("base", b) for b in range(BLOCKS)]
+        raised = [big("raised", b) for b in range(BLOCKS)]
+        ez = [big("ez", b) for b in range(BLOCKS)]
+        result = [big("result", b) for b in range(BLOCKS)]
+        neg_max = [col("neg_max", b) for b in range(BLOCKS)]
+        denom = [col("denom", b) for b in range(BLOCKS)]
+        tz = [col("tz", b) for b in range(BLOCKS)]
+        exp_shift = [col("exp_shift", b) for b in range(BLOCKS)]
+        second_shift = [col("second_shift", b) for b in range(BLOCKS)]
+        first_shift = [col("first_shift", b) for b in range(BLOCKS)]
+
+        for b in range(BLOCKS):
+            nc.vector.tensor_scalar(out=neg_y[b][:], in0=z[b][:], scalar1=-GAIN, scalar2=None, op0=ALU.mult, op1=ALU.min, accum_out=neg_max[b][:])
+            nc.scalar.activation(out=ex[b][:], in_=neg_y[b][:], func=ACT.Exp, scale=-1.0, bias=neg_max[b][:])
+            nc.scalar.activation(out=first_shift[b][:], in_=neg_max[b][:], func=ACT.Copy, scale=-1.0 / GAIN, bias=BITS_BIAS / GAIN)
+            nc.scalar.activation(out=second_shift[b][:], in_=neg_max[b][:], func=ACT.Copy, scale=1.8, bias=-BITS_BIAS)
+            nc.scalar.activation(out=exp_shift[b][:], in_=neg_max[b][:], func=ACT.Copy, scale=1.8)
+        knee = []
+        for b in range(BLOCKS):
+            nc.vector.scalar_tensor_tensor(out=weighted[b][:], in0=labels[b][:], scalar=0.0005, in1=ex[b][:], op0=ALU.add, op1=ALU.mult, accum_out=denom[b][:])
+            knee.append(scaled_log(b, denom[b][:], first_shift[b][:]))
+        for b in range(BLOCKS):
+            nc.vector.scalar_tensor_tensor(out=masked[b][:], in0=labels[b][:], scalar=1.0, in1=neg_mit[b][:], op0=ALU.subtract, op1=ALU.mult)
+            nc.vector.scalar_tensor_tensor(out=base[b][:], in0=z[b][:], scalar=GAIN / KINK, in1=masked[b][:], op0=ALU.mult, op1=ALU.add)
+            nc.vector.scalar_tensor_tensor(out=raised[b][:], in0=z[b][:], scalar=knee[b], in1=base[b][:], op0=ALU.max, op1=ALU.add)
+            nc.scalar.activation(out=ez[b][:], in_=raised[b][:], func=ACT.Exp, scale=KINK, bias=exp_shift[b][:], accum_out=tz[b][:])
+            level = scaled_log(BLOCKS + b, tz[b][:], second_shift[b][:])
+            if b == 0:
+                nc.scalar.activation(out=result[b][:], in_=raised[b][:], func=ACT.Identity, scale=KINK, bias=level)
+            else:
+                nc.vector.tensor_scalar(out=result[b][:], in0=raised[b][:], scalar1=KINK, scalar2=level, op0=ALU.mult, op1=ALU.add)
+            nc.sync.dma_start(out=out[b * P : (b + 1) * P, :], in_=result[b][:])

@@ -2,7 +2,6 @@ import math
 from contextlib import ExitStack
 
 import concourse.mybir as mybir
-from concourse.masks import make_identity
 
 K, T, S, V = 512, 2048, 512, 256
 FLOPS = 2 * K * S * V
@@ -22,9 +21,12 @@ PACK = 4
 BLOCKS = V // P
 CHUNKS = S // P
 ROW = P - 1
+HALF = S // 2
 
 GAIN = 1.2
 KINK = 0.8 * GAIN
+FLOOR = 0.0005
+LIFT = math.log((1.0 + FLOOR) / FLOOR)
 DEG = 16
 LN2 = math.log(2.0)
 BITS_SCALE = LN2 / 2.0**23
@@ -44,25 +46,31 @@ def tile_picked_yseesw_lp_p_kernel(tc, x_words, x_scales, hT, lab, lcnt, lown, o
         count_window = sb.tile([P, T], F32, name="count_window")
         word_window = sb.tile([P, T], I32, name="word_window")
         own = sb.tile([P, BLOCKS], F32, name="own")
-        h_raw = sb.tile([P, PACK, V], F32, name="h_raw")
-        labels = [sb.tile([P, S], F32, name="labels%d" % b) for b in range(BLOCKS)]
 
         nc.vector.memset(scale_window[:].bitcast(I32), 0)
         nc.vector.memset(count_window[0:ROW, 0 : T // 2], 0.0)
-        nc.gpsimd.memset(count_window[0:ROW, T // 2 : T], 0.0)
         nc.sync.dma_start(offsets[:], offs)
         nc.sync.dma_start(out=count_window[ROW:P, :], in_=lcnt[0:1, :])
+        nc.sync.dma_start(out=own[:], in_=lown.rearrange("(p b) o -> p (b o)", b=BLOCKS))
+        nc.sync.dma_start(out=word_window[:], in_=x_words[0].rearrange("p n t -> p (n t)").bitcast(I32))
         for q in range(4):
             nc.sync.dma_start(out=scale_window[32 * q : 32 * q + 4, :].bitcast(I32), in_=x_scales[0, 4 * q : 4 * q + 4, :].bitcast(I32))
-        with nc.allow_non_contiguous_dma(reason="one value a partition"):
-            nc.sync.dma_start(out=own[:], in_=lown.rearrange("(b p) o -> p (b o)", p=P))
-        nc.sync.dma_start(out=word_window[:], in_=x_words[0].rearrange("p n t -> p (n t)").bitcast(I32))
-        nc.sync.dma_start(out=h_raw[:], in_=hT.rearrange("(p j) c -> p j c", j=PACK))
-        for b in range(BLOCKS):
-            nc.sync.dma_start(out=labels[b][:], in_=lab[b * P : (b + 1) * P, :])
 
+        zeros = sb.tile([P, P], F32, name="zeros", tag="late")
         ident = sb.tile([P, P], F32, name="ident")
-        make_identity(nc, ident[:])
+        nc.gpsimd.memset(zeros[:], 0.0)
+        nc.gpsimd.affine_select(out=ident[:], in_=zeros[:], compare_op=ALU.not_equal, fill=1.0, base=0, pattern=[[-1, P]], channel_multiplier=1)
+        nc.gpsimd.memset(count_window[0:ROW, T // 2 : T], 0.0)
+
+        late = sb.tile([P, PACK * V + BLOCKS * S], F32, name="late", tag="late")
+        h_raw = late[:, 0 : PACK * V].rearrange("p (j c) -> p j c", j=PACK)
+        labels = [late[:, PACK * V + b * S : PACK * V + (b + 1) * S] for b in range(BLOCKS)]
+        nc.sync.dma_start(out=late[:, 0 : PACK * V], in_=hT.rearrange("(p j) c -> p (j c)", j=PACK))
+        lab_rows = lab.rearrange("(p b) s -> p b s", b=BLOCKS)
+        out_rows = out.rearrange("(p b) s -> p b s", b=BLOCKS)
+        for b in range(BLOCKS):
+            nc.sync.dma_start(out=labels[b], in_=lab_rows[:, b, :])
+
         one = sb.tile([P, 1], F32, name="one")
         nc.gpsimd.memset(one[:], 1.0)
 
@@ -86,10 +94,12 @@ def tile_picked_yseesw_lp_p_kernel(tc, x_words, x_scales, hT, lab, lcnt, lown, o
 
         counts = sb.tile([P, S], F32, name="counts")
         nc.vector.tensor_copy(out=counts[:], in_=count_window[:].indirect(offsets[:]))
-        x_scale = sb.tile([P, S], U8, name="x_scale", align_bytes=64)
-        nc.vector.tensor_copy(out=x_scale[:], in_=scale_window[:].indirect(offsets[:]))
-        x_codes = sb.tile([P, S], U32, name="x_codes", align_bytes=64)
-        nc.vector.tensor_copy(out=x_codes[:], in_=word_window[:].bitcast(U32).indirect(offsets[:]))
+        x_codes = [sb.tile([P, HALF], U32, name="x_codes%d" % h, align_bytes=64) for h in range(2)]
+        x_scale = [sb.tile([P, HALF], U8, name="x_scale%d" % h, align_bytes=64) for h in range(2)]
+        for h in range(2):
+            picked = offsets[:, h * HALF // 16 : (h + 1) * HALF // 16]
+            nc.vector.tensor_copy(out=x_codes[h][:], in_=word_window[:].bitcast(U32).indirect(picked))
+            nc.vector.tensor_copy(out=x_scale[h][:], in_=scale_window[:].indirect(picked))
 
         own_rows = ps.tile([P, V], F32, name="own_rows")
         for b in range(BLOCKS):
@@ -105,23 +115,28 @@ def tile_picked_yseesw_lp_p_kernel(tc, x_words, x_scales, hT, lab, lcnt, lown, o
         for b in range(BLOCKS):
             for c in range(CHUNKS):
                 nc.tensor.matmul(neg_mit[b][:, c * P : (c + 1) * P], lhsT=cap_col[:, c : c + 1].to_broadcast([P, P]), rhs=ident[:], is_transpose=True, start=(c == 0), stop=False)
-        for c in range(CHUNKS):
-            short_t = sb.tile([P, V], F32, name="short_t%d" % c)
-            nc.scalar.activation(out=short_t[:], in_=own_rows[:], func=ACT.Relu, scale=-1.0 / KINK, bias=gap_col[:, c : c + 1])
-            for b in range(BLOCKS):
-                nc.tensor.matmul(neg_mit[b][:, c * P : (c + 1) * P], lhsT=short_t[:, b * P : (b + 1) * P], rhs=ident[:], is_transpose=True, start=False, stop=(c == CHUNKS - 1))
 
-        grouped = [sb.tile([P, P, PACK], BF16, name="grouped%d" % b, align_bytes=64) for b in range(BLOCKS)]
-        nc.vector.tensor_copy(out=grouped[0][:], in_=h_raw[:, :, 0:P].rearrange("p j c -> p c j"))
-        nc.scalar.copy(out=grouped[1][:], in_=h_raw[:, :, P : 2 * P].rearrange("p j c -> p c j"))
+        def add_shortfall(b, tag):
+            short_t = sb.tile([P, S], F32, name="short_t%d" % b, tag=tag, align_bytes=64)
+            for c in range(CHUNKS):
+                cols = slice(c * P, (c + 1) * P)
+                nc.scalar.activation(out=short_t[:, cols], in_=own_rows[:, b * P : (b + 1) * P], func=ACT.Relu, scale=-1.0 / KINK, bias=gap_col[:, c : c + 1])
+                nc.tensor.matmul(neg_mit[b][:, cols], lhsT=short_t[:, cols], rhs=ident[:], is_transpose=True, start=False, stop=(c == CHUNKS - 1))
+
+        add_shortfall(0, "short_t0")
+
+        grouped = [sb.tile([P, P, PACK], BF16, name="grouped%d" % b, tag="grouped%d" % b, align_bytes=64) for b in range(BLOCKS)]
         z = []
         for b in range(BLOCKS):
+            nc.scalar.copy(out=grouped[b][:], in_=h_raw[:, :, b:V:BLOCKS].rearrange("p j c -> p c j"))
             h_codes = sb.tile([P, P], U32, name="h_codes%d" % b, align_bytes=64)
             h_scale = sb.tile([P, P], U8, name="h_scale%d" % b, align_bytes=64)
             nc.vector.quantize_mx(out=h_codes[:].bitcast(FP8X4), scales=h_scale[:], in_=grouped[b][:].rearrange("p c j -> p (c j)"))
             zb = ps.tile([P, S], F32, name="z%d" % b)
-            nc.tensor.matmul_mx(out=zb[:], lhsT=h_codes[:].bitcast(FP8X4), lhsT_scale=h_scale[:], rhs=x_codes[:].bitcast(FP8X4), rhs_scale=x_scale[:], start=True, stop=True)
+            for h in range(2):
+                nc.tensor.matmul_mx(out=zb[:, h * HALF : (h + 1) * HALF], lhsT=h_codes[:].bitcast(FP8X4), lhsT_scale=h_scale[:], rhs=x_codes[h][:].bitcast(FP8X4), rhs_scale=x_scale[h][:], start=True, stop=True)
             z.append(zb)
+        add_shortfall(1, "grouped1")
 
         def big(name, b):
             return sb.tile([P, S], F32, name="%s%d" % (name, b))
@@ -144,24 +159,27 @@ def tile_picked_yseesw_lp_p_kernel(tc, x_words, x_scales, hT, lab, lcnt, lown, o
         second_shift = [col("second_shift", b) for b in range(BLOCKS)]
         first_shift = [col("first_shift", b) for b in range(BLOCKS)]
 
-        for b in range(BLOCKS):
-            nc.vector.tensor_scalar(out=neg_y[b][:], in0=z[b][:], scalar1=-GAIN, scalar2=None, op0=ALU.mult, op1=ALU.min, accum_out=neg_max[b][:])
-            nc.scalar.activation(out=ex[b][:], in_=neg_y[b][:], func=ACT.Exp, scale=-1.0, bias=neg_max[b][:])
-            nc.scalar.activation(out=first_shift[b][:], in_=neg_max[b][:], func=ACT.Copy, scale=-1.0 / GAIN, bias=BITS_BIAS / GAIN)
-            nc.scalar.activation(out=second_shift[b][:], in_=neg_max[b][:], func=ACT.Copy, scale=1.8, bias=-BITS_BIAS)
-            nc.scalar.activation(out=exp_shift[b][:], in_=neg_max[b][:], func=ACT.Copy, scale=1.8)
         knee = []
         for b in range(BLOCKS):
-            nc.vector.scalar_tensor_tensor(out=weighted[b][:], in0=labels[b][:], scalar=0.0005, in1=ex[b][:], op0=ALU.add, op1=ALU.mult, accum_out=denom[b][:])
+            nc.vector.tensor_scalar(out=neg_y[b][:], in0=z[b][:], scalar1=-GAIN, scalar2=None, op0=ALU.mult, op1=ALU.min, accum_out=neg_max[b][:])
+            nc.vector.scalar_tensor_tensor(out=weighted[b][:], in0=labels[b], scalar=LIFT / GAIN, in1=z[b][:], op0=ALU.mult, op1=ALU.add)
+            nc.scalar.activation(out=first_shift[b][:], in_=neg_max[b][:], func=ACT.Copy, scale=-1.0 / GAIN, bias=(BITS_BIAS + math.log(FLOOR)) / GAIN)
+            nc.scalar.activation(out=second_shift[b][:], in_=neg_max[b][:], func=ACT.Copy, scale=1.8, bias=-BITS_BIAS)
+            nc.scalar.activation(out=exp_shift[b][:], in_=neg_max[b][:], func=ACT.Copy, scale=1.8)
+            nc.scalar.activation(out=ex[b][:], in_=weighted[b][:], func=ACT.Exp, scale=GAIN, bias=neg_max[b][:], accum_out=denom[b][:])
             knee.append(scaled_log(b, denom[b][:], first_shift[b][:]))
         for b in range(BLOCKS):
-            nc.vector.scalar_tensor_tensor(out=masked[b][:], in0=labels[b][:], scalar=1.0, in1=neg_mit[b][:], op0=ALU.subtract, op1=ALU.mult)
+            nc.vector.scalar_tensor_tensor(out=masked[b][:], in0=labels[b], scalar=1.0, in1=neg_mit[b][:], op0=ALU.subtract, op1=ALU.mult)
             nc.vector.scalar_tensor_tensor(out=base[b][:], in0=z[b][:], scalar=GAIN / KINK, in1=masked[b][:], op0=ALU.mult, op1=ALU.add)
             nc.vector.scalar_tensor_tensor(out=raised[b][:], in0=z[b][:], scalar=knee[b], in1=base[b][:], op0=ALU.max, op1=ALU.add)
             nc.scalar.activation(out=ez[b][:], in_=raised[b][:], func=ACT.Exp, scale=KINK, bias=exp_shift[b][:], accum_out=tz[b][:])
             level = scaled_log(BLOCKS + b, tz[b][:], second_shift[b][:])
             if b == 0:
                 nc.scalar.activation(out=result[b][:], in_=raised[b][:], func=ACT.Identity, scale=KINK, bias=level)
+                nc.sync.dma_start(out=out_rows[:, b, :], in_=result[b][:])
             else:
-                nc.vector.tensor_scalar(out=result[b][:], in0=raised[b][:], scalar1=KINK, scalar2=level, op0=ALU.mult, op1=ALU.add)
-            nc.sync.dma_start(out=out[b * P : (b + 1) * P, :], in_=result[b][:])
+                for h in range(2):
+                    cols = slice(h * HALF, (h + 1) * HALF)
+                    nc.vector.tensor_scalar(out=result[b][:, cols], in0=raised[b][:, cols], scalar1=KINK, scalar2=level, op0=ALU.mult, op1=ALU.add)
+                    queue = nc.sync if h == 0 else nc.scalar
+                    queue.dma_start(out=out_rows[:, b, cols], in_=result[b][:, cols])

@@ -145,7 +145,6 @@ def tile_picked_yseesw_lp_p_kernel(tc, x_words, x_scales, hT, lab, lcnt, lown, o
             return sb.tile([P, 1], F32, name="%s%d" % (name, b))
 
         masked = [big("masked", b) for b in range(BLOCKS)]
-        neg_y = [big("neg_y", b) for b in range(BLOCKS)]
         ex = [big("ex", b) for b in range(BLOCKS)]
         weighted = [big("weighted", b) for b in range(BLOCKS)]
         base = [big("base", b) for b in range(BLOCKS)]
@@ -159,18 +158,30 @@ def tile_picked_yseesw_lp_p_kernel(tc, x_words, x_scales, hT, lab, lcnt, lown, o
         second_shift = [col("second_shift", b) for b in range(BLOCKS)]
         first_shift = [col("first_shift", b) for b in range(BLOCKS)]
 
+        def mask(b):
+            nc.vector.scalar_tensor_tensor(out=masked[b][:], in0=labels[b], scalar=1.0, in1=neg_mit[b][:], op0=ALU.subtract, op1=ALU.mult)
+
+        mask(0)
+        neg_scaled = sb.tile([P, S], F32, name="neg_scaled")
+        peak = [col("peak", b) for b in range(BLOCKS)]
+        to_neg_max = [KINK, -GAIN]
         knee = []
         for b in range(BLOCKS):
-            nc.vector.tensor_scalar(out=neg_y[b][:], in0=z[b][:], scalar1=-GAIN, scalar2=None, op0=ALU.mult, op1=ALU.min, accum_out=neg_max[b][:])
+            if b == 0:
+                nc.vector.tensor_scalar(out=neg_scaled[:], in0=z[b][:], scalar1=-GAIN / KINK, scalar2=None, op0=ALU.mult, op1=ALU.min, accum_out=peak[b][:])
+                nc.gpsimd.tensor_tensor(out=base[b][:], in0=masked[b][:], in1=neg_scaled[:], op=ALU.subtract)
+            else:
+                nc.vector.tensor_reduce(out=peak[b][:], in_=z[b][:], axis=mybir.AxisListType.X, op=ALU.max)
             nc.vector.scalar_tensor_tensor(out=weighted[b][:], in0=labels[b], scalar=LIFT / GAIN, in1=z[b][:], op0=ALU.mult, op1=ALU.add)
-            nc.scalar.activation(out=first_shift[b][:], in_=neg_max[b][:], func=ACT.Copy, scale=-1.0 / GAIN, bias=(BITS_BIAS + math.log(FLOOR)) / GAIN)
-            nc.scalar.activation(out=second_shift[b][:], in_=neg_max[b][:], func=ACT.Copy, scale=1.8, bias=-BITS_BIAS)
-            nc.scalar.activation(out=exp_shift[b][:], in_=neg_max[b][:], func=ACT.Copy, scale=1.8)
+            nc.scalar.activation(out=neg_max[b][:], in_=peak[b][:], func=ACT.Copy, scale=to_neg_max[b])
+            nc.scalar.activation(out=first_shift[b][:], in_=peak[b][:], func=ACT.Copy, scale=-to_neg_max[b] / GAIN, bias=(BITS_BIAS + math.log(FLOOR)) / GAIN)
+            nc.scalar.activation(out=second_shift[b][:], in_=peak[b][:], func=ACT.Copy, scale=1.8 * to_neg_max[b], bias=-BITS_BIAS)
+            nc.scalar.activation(out=exp_shift[b][:], in_=peak[b][:], func=ACT.Copy, scale=1.8 * to_neg_max[b])
             nc.scalar.activation(out=ex[b][:], in_=weighted[b][:], func=ACT.Exp, scale=GAIN, bias=neg_max[b][:], accum_out=denom[b][:])
             knee.append(scaled_log(b, denom[b][:], first_shift[b][:]))
+        mask(1)
+        nc.vector.scalar_tensor_tensor(out=base[1][:], in0=z[1][:], scalar=GAIN / KINK, in1=masked[1][:], op0=ALU.mult, op1=ALU.add)
         for b in range(BLOCKS):
-            nc.vector.scalar_tensor_tensor(out=masked[b][:], in0=labels[b], scalar=1.0, in1=neg_mit[b][:], op0=ALU.subtract, op1=ALU.mult)
-            nc.vector.scalar_tensor_tensor(out=base[b][:], in0=z[b][:], scalar=GAIN / KINK, in1=masked[b][:], op0=ALU.mult, op1=ALU.add)
             nc.vector.scalar_tensor_tensor(out=raised[b][:], in0=z[b][:], scalar=knee[b], in1=base[b][:], op0=ALU.max, op1=ALU.add)
             nc.scalar.activation(out=ez[b][:], in_=raised[b][:], func=ACT.Exp, scale=KINK, bias=exp_shift[b][:], accum_out=tz[b][:])
             level = scaled_log(BLOCKS + b, tz[b][:], second_shift[b][:])

@@ -87,7 +87,10 @@ def tile_picked_yseesw_lp_p_kernel(tc, x_words, x_scales, hT, lab, lcnt, lown, o
             inverse = sb.tile([P, 1], F32, name="inverse%d" % n)
             nc.scalar.activation(out=inverse[:], in_=bits, func=ACT.Exp, scale=-BITS_SCALE, bias=-BITS_BIAS)
             nc.scalar.activation(out=addends[:, n, DEG:STEPS], in_=bits, func=ACT.Identity, scale=gains[n // BLOCKS] * BITS_SCALE, bias=shift)
-            nc.scalar.activation(out=factors[n][:, 0:DEG], in_=inverse[:].to_broadcast([P, DEG]), func=ACT.Copy, scale=total, bias=-1.0)
+            if n < BLOCKS:
+                nc.scalar.activation(out=factors[n][:, 0:DEG], in_=inverse[:].to_broadcast([P, DEG]), func=ACT.Copy, scale=total, bias=-1.0)
+            else:
+                nc.vector.tensor_scalar(out=factors[n][:, 0:DEG], in0=inverse[:].to_broadcast([P, DEG]), scalar1=total, scalar2=-1.0, op0=ALU.mult, op1=ALU.add)
             horner = sb.tile([P, STEPS], F32, name="horner%d" % n)
             nc.vector.tensor_tensor_scan(out=horner[:], data0=factors[n][:], data1=addends[:, n, 0:STEPS], initial=POLY[DEG], op0=ALU.mult, op1=ALU.add)
             return horner[:, STEPS - 1 : STEPS]
@@ -186,7 +189,7 @@ def tile_picked_yseesw_lp_p_kernel(tc, x_words, x_scales, hT, lab, lcnt, lown, o
             nc.scalar.activation(out=ez[b][:], in_=raised[b][:], func=ACT.Exp, scale=KINK, bias=exp_shift[b][:], accum_out=tz[b][:])
             level = scaled_log(BLOCKS + b, tz[b][:], second_shift[b][:])
             if b == 0:
-                nc.scalar.activation(out=result[b][:], in_=raised[b][:], func=ACT.Identity, scale=KINK, bias=level)
+                nc.vector.tensor_scalar(out=result[b][:], in0=raised[b][:], scalar1=KINK, scalar2=level, op0=ALU.mult, op1=ALU.add)
                 nc.sync.dma_start(out=out_rows[:, b, :], in_=result[b][:])
             else:
                 for h in range(2):

@@ -18,6 +18,8 @@ ACT = mybir.ActivationFunctionType
 
 P = 128
 PACK = 4
+QUADRANTS = 4
+LIST_ROWS = 16
 BLOCKS = V // P
 CHUNKS = S // P
 ROW = P - 1
@@ -25,14 +27,18 @@ HALF = S // 2
 
 GAIN = 1.2
 KINK = 0.8 * GAIN
+BOTH = 1.0 + 0.8
 FLOOR = 0.0005
 LIFT = math.log((1.0 + FLOOR) / FLOOR)
-DEG = 16
-LN2 = math.log(2.0)
-BITS_SCALE = LN2 / 2.0**23
+
+BITS_SCALE = math.log(2.0) / 2.0**23
 BITS_BIAS = -88.0
-POLY = [0.0] + [(-1.0) ** (n + 1) / n for n in range(1, DEG + 1)]
+DEG = 16
+SERIES = [0.0] + [(-1.0) ** (n + 1) / n for n in range(1, DEG + 1)]
 STEPS = DEG + 1
+STEPS_PADDED = 24
+LOGS = 2 * BLOCKS
+LOG_GAINS = [1.0 / GAIN] * BLOCKS + [-1.0] * BLOCKS
 
 
 def tile_picked_yseesw_lp_p_kernel(tc, x_words, x_scales, hT, lab, lcnt, lown, offs, out):
@@ -41,7 +47,7 @@ def tile_picked_yseesw_lp_p_kernel(tc, x_words, x_scales, hT, lab, lcnt, lown, o
         sb = ctx.enter_context(tc.tile_pool(name="sb", bufs=1))
         ps = ctx.enter_context(tc.psum_pool(name="ps", bufs=1))
 
-        offsets = sb.tile([P, S // 16], U16, name="offsets")
+        offsets = sb.tile([P, S // LIST_ROWS], U16, name="offsets")
         scale_window = sb.tile([P, T], U8, name="scale_window")
         count_window = sb.tile([P, T], F32, name="count_window")
         word_window = sb.tile([P, T], I32, name="word_window")
@@ -53,13 +59,18 @@ def tile_picked_yseesw_lp_p_kernel(tc, x_words, x_scales, hT, lab, lcnt, lown, o
         nc.sync.dma_start(out=count_window[ROW:P, :], in_=lcnt[0:1, :])
         nc.sync.dma_start(out=own[:], in_=lown.rearrange("(p b) o -> p (b o)", b=BLOCKS))
         nc.sync.dma_start(out=word_window[:], in_=x_words[0].rearrange("p n t -> p (n t)").bitcast(I32))
-        for q in range(4):
-            nc.sync.dma_start(out=scale_window[32 * q : 32 * q + 4, :].bitcast(I32), in_=x_scales[0, 4 * q : 4 * q + 4, :].bitcast(I32))
+        for q in range(QUADRANTS):
+            nc.sync.dma_start(
+                out=scale_window[32 * q : 32 * q + 4, :].bitcast(I32),
+                in_=x_scales[0, 4 * q : 4 * q + 4, :].bitcast(I32),
+            )
 
         zeros = sb.tile([P, P], F32, name="zeros", tag="late")
         ident = sb.tile([P, P], F32, name="ident")
         nc.gpsimd.memset(zeros[:], 0.0)
-        nc.gpsimd.affine_select(out=ident[:], in_=zeros[:], compare_op=ALU.not_equal, fill=1.0, base=0, pattern=[[-1, P]], channel_multiplier=1)
+        nc.gpsimd.affine_select(
+            out=ident[:], in_=zeros[:], compare_op=ALU.not_equal, fill=1.0, base=0, pattern=[[-1, P]], channel_multiplier=1
+        )
         nc.gpsimd.memset(count_window[0:ROW, T // 2 : T], 0.0)
 
         late = sb.tile([P, PACK * V + BLOCKS * S], F32, name="late", tag="late")
@@ -74,33 +85,35 @@ def tile_picked_yseesw_lp_p_kernel(tc, x_words, x_scales, hT, lab, lcnt, lown, o
         one = sb.tile([P, 1], F32, name="one")
         nc.gpsimd.memset(one[:], 1.0)
 
-        addends = sb.tile([P, 2 * BLOCKS, 24], F32, name="addends")
+        addends = sb.tile([P, LOGS, STEPS_PADDED], F32, name="addends")
         for i in range(DEG):
-            nc.scalar.activation(out=addends[:, :, DEG - 1 - i], in_=one[:].to_broadcast([P, 2 * BLOCKS]), func=ACT.Copy, scale=POLY[i])
-        gains = [1.0 / GAIN, -1.0]
-        factors = [sb.tile([P, STEPS], F32, name="factors%d" % n) for n in range(2 * BLOCKS)]
-        for n in range(2 * BLOCKS):
-            nc.scalar.activation(out=factors[n][:, STEPS - 1 : STEPS], in_=one[:], func=ACT.Copy, scale=gains[n // BLOCKS])
+            nc.scalar.activation(out=addends[:, :, DEG - 1 - i], in_=one[:].to_broadcast([P, LOGS]), func=ACT.Copy, scale=SERIES[i])
+        factors = [sb.tile([P, STEPS], F32, name="factors%d" % n) for n in range(LOGS)]
+        for n in range(LOGS):
+            nc.scalar.activation(out=factors[n][:, DEG:STEPS], in_=one[:], func=ACT.Copy, scale=LOG_GAINS[n])
 
         def scaled_log(n, total, shift):
             bits = total.bitcast(U32)
             inverse = sb.tile([P, 1], F32, name="inverse%d" % n)
             nc.scalar.activation(out=inverse[:], in_=bits, func=ACT.Exp, scale=-BITS_SCALE, bias=-BITS_BIAS)
-            nc.scalar.activation(out=addends[:, n, DEG:STEPS], in_=bits, func=ACT.Identity, scale=gains[n // BLOCKS] * BITS_SCALE, bias=shift)
-            if n < BLOCKS:
-                nc.scalar.activation(out=factors[n][:, 0:DEG], in_=inverse[:].to_broadcast([P, DEG]), func=ACT.Copy, scale=total, bias=-1.0)
+            nc.scalar.activation(out=addends[:, n, DEG:STEPS], in_=bits, func=ACT.Identity, scale=LOG_GAINS[n] * BITS_SCALE, bias=shift)
+            repeated = inverse[:].to_broadcast([P, DEG])
+            if n == BLOCKS:
+                nc.vector.tensor_scalar(out=factors[n][:, 0:DEG], in0=repeated, scalar1=total, scalar2=-1.0, op0=ALU.mult, op1=ALU.add)
             else:
-                nc.vector.tensor_scalar(out=factors[n][:, 0:DEG], in0=inverse[:].to_broadcast([P, DEG]), scalar1=total, scalar2=-1.0, op0=ALU.mult, op1=ALU.add)
+                nc.scalar.activation(out=factors[n][:, 0:DEG], in_=repeated, func=ACT.Copy, scale=total, bias=-1.0)
             horner = sb.tile([P, STEPS], F32, name="horner%d" % n)
-            nc.vector.tensor_tensor_scan(out=horner[:], data0=factors[n][:], data1=addends[:, n, 0:STEPS], initial=POLY[DEG], op0=ALU.mult, op1=ALU.add)
-            return horner[:, STEPS - 1 : STEPS]
+            nc.vector.tensor_tensor_scan(
+                out=horner[:], data0=factors[n][:], data1=addends[:, n, 0:STEPS], initial=SERIES[DEG], op0=ALU.mult, op1=ALU.add
+            )
+            return horner[:, DEG:STEPS]
 
         counts = sb.tile([P, S], F32, name="counts")
         nc.vector.tensor_copy(out=counts[:], in_=count_window[:].indirect(offsets[:]))
         x_codes = [sb.tile([P, HALF], U32, name="x_codes%d" % h, align_bytes=64) for h in range(2)]
         x_scale = [sb.tile([P, HALF], U8, name="x_scale%d" % h, align_bytes=64) for h in range(2)]
         for h in range(2):
-            picked = offsets[:, h * HALF // 16 : (h + 1) * HALF // 16]
+            picked = offsets[:, h * HALF // LIST_ROWS : (h + 1) * HALF // LIST_ROWS]
             nc.vector.tensor_copy(out=x_codes[h][:], in_=word_window[:].bitcast(U32).indirect(picked))
             nc.vector.tensor_copy(out=x_scale[h][:], in_=scale_window[:].indirect(picked))
 
@@ -112,18 +125,27 @@ def tile_picked_yseesw_lp_p_kernel(tc, x_words, x_scales, hT, lab, lcnt, lown, o
             nc.tensor.transpose(counts_t[:, c, :], counts[:, c * P : (c + 1) * P], ident[:])
         gap_col = sb.tile([P, CHUNKS], F32, name="gap_col")
         cap_col = sb.tile([P, CHUNKS], F32, name="cap_col")
-        nc.scalar.activation(out=gap_col[:], in_=counts_t[:, :, ROW], func=ACT.Copy, scale=-0.45 / KINK)
+        nc.scalar.activation(out=gap_col[:], in_=counts_t[:, :, ROW], func=ACT.Copy, scale=-(0.5 - 0.05) / KINK)
         nc.scalar.activation(out=cap_col[:], in_=counts_t[:, :, ROW], func=ACT.Copy, scale=-0.05 / KINK)
         neg_mit = [ps.tile([P, S], F32, name="neg_mit%d" % b) for b in range(BLOCKS)]
         for b in range(BLOCKS):
             for c in range(CHUNKS):
-                nc.tensor.matmul(neg_mit[b][:, c * P : (c + 1) * P], lhsT=cap_col[:, c : c + 1].to_broadcast([P, P]), rhs=ident[:], is_transpose=True, start=(c == 0), stop=False)
+                nc.tensor.matmul(
+                    neg_mit[b][:, c * P : (c + 1) * P],
+                    lhsT=cap_col[:, c : c + 1].to_broadcast([P, P]),
+                    rhs=ident[:],
+                    is_transpose=True,
+                    start=(c == 0),
+                    stop=False,
+                )
 
         def add_shortfall(b, tag):
             short_t = sb.tile([P, S], F32, name="short_t%d" % b, tag=tag, align_bytes=64)
             for c in range(CHUNKS):
                 cols = slice(c * P, (c + 1) * P)
-                nc.scalar.activation(out=short_t[:, cols], in_=own_rows[:, b * P : (b + 1) * P], func=ACT.Relu, scale=-1.0 / KINK, bias=gap_col[:, c : c + 1])
+                nc.scalar.activation(
+                    out=short_t[:, cols], in_=own_rows[:, b * P : (b + 1) * P], func=ACT.Relu, scale=-1.0 / KINK, bias=gap_col[:, c : c + 1]
+                )
                 nc.tensor.matmul(neg_mit[b][:, cols], lhsT=short_t[:, cols], rhs=ident[:], is_transpose=True, start=False, stop=(c == CHUNKS - 1))
 
         add_shortfall(0, "short_t0")
@@ -135,65 +157,77 @@ def tile_picked_yseesw_lp_p_kernel(tc, x_words, x_scales, hT, lab, lcnt, lown, o
             h_codes = sb.tile([P, P], U32, name="h_codes%d" % b, align_bytes=64)
             h_scale = sb.tile([P, P], U8, name="h_scale%d" % b, align_bytes=64)
             nc.vector.quantize_mx(out=h_codes[:].bitcast(FP8X4), scales=h_scale[:], in_=grouped[b][:].rearrange("p c j -> p (c j)"))
-            zb = ps.tile([P, S], F32, name="z%d" % b)
+            product = ps.tile([P, S], F32, name="z%d" % b)
             for h in range(2):
-                nc.tensor.matmul_mx(out=zb[:, h * HALF : (h + 1) * HALF], lhsT=h_codes[:].bitcast(FP8X4), lhsT_scale=h_scale[:], rhs=x_codes[h][:].bitcast(FP8X4), rhs_scale=x_scale[h][:], start=True, stop=True)
-            z.append(zb)
+                nc.tensor.matmul_mx(
+                    out=product[:, h * HALF : (h + 1) * HALF],
+                    lhsT=h_codes[:].bitcast(FP8X4),
+                    lhsT_scale=h_scale[:],
+                    rhs=x_codes[h][:].bitcast(FP8X4),
+                    rhs_scale=x_scale[h][:],
+                    start=True,
+                    stop=True,
+                )
+            z.append(product)
         add_shortfall(1, "grouped1")
 
-        def big(name, b):
+        def wide(name, b):
             return sb.tile([P, S], F32, name="%s%d" % (name, b))
 
-        def col(name, b):
+        def column(name, b):
             return sb.tile([P, 1], F32, name="%s%d" % (name, b))
 
-        masked = [big("masked", b) for b in range(BLOCKS)]
-        ex = [big("ex", b) for b in range(BLOCKS)]
-        weighted = [big("weighted", b) for b in range(BLOCKS)]
-        base = [big("base", b) for b in range(BLOCKS)]
-        raised = [big("raised", b) for b in range(BLOCKS)]
-        ez = [big("ez", b) for b in range(BLOCKS)]
-        result = [big("result", b) for b in range(BLOCKS)]
-        neg_max = [col("neg_max", b) for b in range(BLOCKS)]
-        denom = [col("denom", b) for b in range(BLOCKS)]
-        tz = [col("tz", b) for b in range(BLOCKS)]
-        exp_shift = [col("exp_shift", b) for b in range(BLOCKS)]
-        second_shift = [col("second_shift", b) for b in range(BLOCKS)]
-        first_shift = [col("first_shift", b) for b in range(BLOCKS)]
+        masked = [wide("masked", b) for b in range(BLOCKS)]
+        ex = [wide("ex", b) for b in range(BLOCKS)]
+        lifted = [wide("lifted", b) for b in range(BLOCKS)]
+        base = [wide("base", b) for b in range(BLOCKS)]
+        raised = [wide("raised", b) for b in range(BLOCKS)]
+        result = [wide("result", b) for b in range(BLOCKS)]
+        neg_max = [column("neg_max", b) for b in range(BLOCKS)]
+        denom = [column("denom", b) for b in range(BLOCKS)]
+        tz = [column("tz", b) for b in range(BLOCKS)]
+        exp_shift = [column("exp_shift", b) for b in range(BLOCKS)]
+        second_shift = [sb.tile([P, 1], F32, name="second_shift%d" % b, tag="second_shift%d" % b) for b in range(BLOCKS)]
+        first_shift = [column("first_shift", b) for b in range(BLOCKS)]
 
         def mask(b):
             nc.vector.scalar_tensor_tensor(out=masked[b][:], in0=labels[b], scalar=1.0, in1=neg_mit[b][:], op0=ALU.subtract, op1=ALU.mult)
 
         mask(0)
         neg_scaled = sb.tile([P, S], F32, name="neg_scaled")
-        peak = [col("peak", b) for b in range(BLOCKS)]
+        peak = [column("peak", b) for b in range(BLOCKS)]
         to_neg_max = [KINK, -GAIN]
         knee = []
         for b in range(BLOCKS):
             if b == 0:
-                nc.vector.tensor_scalar(out=neg_scaled[:], in0=z[b][:], scalar1=-GAIN / KINK, scalar2=None, op0=ALU.mult, op1=ALU.min, accum_out=peak[b][:])
+                nc.vector.tensor_scalar(
+                    out=neg_scaled[:], in0=z[b][:], scalar1=-GAIN / KINK, scalar2=None, op0=ALU.mult, op1=ALU.min, accum_out=peak[b][:]
+                )
                 nc.gpsimd.tensor_tensor(out=base[b][:], in0=masked[b][:], in1=neg_scaled[:], op=ALU.subtract)
             else:
                 nc.vector.tensor_reduce(out=peak[b][:], in_=z[b][:], axis=mybir.AxisListType.X, op=ALU.max)
-            nc.vector.scalar_tensor_tensor(out=weighted[b][:], in0=labels[b], scalar=LIFT / GAIN, in1=z[b][:], op0=ALU.mult, op1=ALU.add)
+            nc.vector.scalar_tensor_tensor(out=lifted[b][:], in0=labels[b], scalar=LIFT / GAIN, in1=z[b][:], op0=ALU.mult, op1=ALU.add)
             nc.scalar.activation(out=neg_max[b][:], in_=peak[b][:], func=ACT.Copy, scale=to_neg_max[b])
-            nc.scalar.activation(out=first_shift[b][:], in_=peak[b][:], func=ACT.Copy, scale=-to_neg_max[b] / GAIN, bias=(BITS_BIAS + math.log(FLOOR)) / GAIN)
-            nc.scalar.activation(out=second_shift[b][:], in_=peak[b][:], func=ACT.Copy, scale=1.8 * to_neg_max[b], bias=-BITS_BIAS)
-            nc.scalar.activation(out=exp_shift[b][:], in_=peak[b][:], func=ACT.Copy, scale=1.8 * to_neg_max[b])
-            nc.scalar.activation(out=ex[b][:], in_=weighted[b][:], func=ACT.Exp, scale=GAIN, bias=neg_max[b][:], accum_out=denom[b][:])
+            nc.scalar.activation(
+                out=first_shift[b][:], in_=peak[b][:], func=ACT.Copy, scale=-to_neg_max[b] / GAIN, bias=(BITS_BIAS + math.log(FLOOR)) / GAIN
+            )
+            nc.scalar.activation(out=second_shift[b][:], in_=peak[b][:], func=ACT.Copy, scale=BOTH * to_neg_max[b], bias=-BITS_BIAS)
+            nc.scalar.activation(out=exp_shift[b][:], in_=peak[b][:], func=ACT.Copy, scale=BOTH * to_neg_max[b])
+            nc.scalar.activation(out=ex[b][:], in_=lifted[b][:], func=ACT.Exp, scale=GAIN, bias=neg_max[b][:], accum_out=denom[b][:])
             knee.append(scaled_log(b, denom[b][:], first_shift[b][:]))
         mask(1)
         nc.vector.scalar_tensor_tensor(out=base[1][:], in0=z[1][:], scalar=GAIN / KINK, in1=masked[1][:], op0=ALU.mult, op1=ALU.add)
+
+        ez_tags = ["ez0", "second_shift0"]
         for b in range(BLOCKS):
             nc.vector.scalar_tensor_tensor(out=raised[b][:], in0=z[b][:], scalar=knee[b], in1=base[b][:], op0=ALU.max, op1=ALU.add)
-            nc.scalar.activation(out=ez[b][:], in_=raised[b][:], func=ACT.Exp, scale=KINK, bias=exp_shift[b][:], accum_out=tz[b][:])
+            ez = sb.tile([P, S], F32, name="ez%d" % b, tag=ez_tags[b])
+            nc.scalar.activation(out=ez[:], in_=raised[b][:], func=ACT.Exp, scale=KINK, bias=exp_shift[b][:], accum_out=tz[b][:])
             level = scaled_log(BLOCKS + b, tz[b][:], second_shift[b][:])
             if b == 0:
-                nc.vector.tensor_scalar(out=result[b][:], in0=raised[b][:], scalar1=KINK, scalar2=level, op0=ALU.mult, op1=ALU.add)
-                nc.sync.dma_start(out=out_rows[:, b, :], in_=result[b][:])
+                pieces = [(slice(0, S), nc.sync)]
             else:
-                for h in range(2):
-                    cols = slice(h * HALF, (h + 1) * HALF)
-                    nc.vector.tensor_scalar(out=result[b][:, cols], in0=raised[b][:, cols], scalar1=KINK, scalar2=level, op0=ALU.mult, op1=ALU.add)
-                    queue = nc.sync if h == 0 else nc.scalar
-                    queue.dma_start(out=out_rows[:, b, cols], in_=result[b][:, cols])
+                pieces = [(slice(0, HALF), nc.sync), (slice(HALF, S), nc.scalar)]
+            for cols, queue in pieces:
+                nc.vector.tensor_scalar(out=result[b][:, cols], in0=raised[b][:, cols], scalar1=KINK, scalar2=level, op0=ALU.mult, op1=ALU.add)
+                queue.dma_start(out=out_rows[:, b, cols], in_=result[b][:, cols])

import math
from contextlib import ExitStack

import concourse.mybir as mybir

K, T, S, V = 512, 2048, 512, 256
FLOPS = 2 * K * S * V

F32 = mybir.dt.float32
BF16 = mybir.dt.bfloat16
I32 = mybir.dt.int32
U32 = mybir.dt.uint32
U16 = mybir.dt.uint16
U8 = mybir.dt.uint8
FP8X4 = mybir.dt.float8_e4m3fn_x4
ALU = mybir.AluOpType
ACT = mybir.ActivationFunctionType

P = 128
PACK = 4
QUADRANTS = 4
LIST_ROWS = 16
BLOCKS = V // P
CHUNKS = S // P
ROW = P - 1
HALF = S // 2

GAIN = 1.2
KINK = 0.8 * GAIN
BOTH = 1.0 + 0.8
FLOOR = 0.0005
LIFT = math.log((1.0 + FLOOR) / FLOOR)

BITS_SCALE = math.log(2.0) / 2.0**23
BITS_BIAS = -88.0
DEG = 16
SERIES = [0.0] + [(-1.0) ** (n + 1) / n for n in range(1, DEG + 1)]
STEPS = DEG + 1
STEPS_PADDED = 24
LOGS = 2 * BLOCKS
LOG_GAINS = [1.0 / GAIN] * BLOCKS + [-1.0] * BLOCKS


def tile_picked_yseesw_lp_p_kernel(tc, x_words, x_scales, hT, lab, lcnt, lown, offs, out):
    nc = tc.nc
    with ExitStack() as ctx:
        sb = ctx.enter_context(tc.tile_pool(name="sb", bufs=1))
        ps = ctx.enter_context(tc.psum_pool(name="ps", bufs=1))

        offsets = sb.tile([P, S // LIST_ROWS], U16, name="offsets")
        scale_window = sb.tile([P, T], U8, name="scale_window")
        count_window = sb.tile([P, T], F32, name="count_window")
        word_window = sb.tile([P, T], I32, name="word_window")
        own = sb.tile([P, BLOCKS], F32, name="own")

        nc.vector.memset(scale_window[:].bitcast(I32), 0)
        nc.vector.memset(count_window[0:ROW, 0 : T // 2], 0.0)
        nc.sync.dma_start(offsets[:], offs)
        nc.sync.dma_start(out=count_window[ROW:P, :], in_=lcnt[0:1, :])
        nc.sync.dma_start(out=own[:], in_=lown.rearrange("(p b) o -> p (b o)", b=BLOCKS))
        nc.sync.dma_start(out=word_window[:], in_=x_words[0].rearrange("p n t -> p (n t)").bitcast(I32))
        for q in range(QUADRANTS):
            nc.sync.dma_start(
                out=scale_window[32 * q : 32 * q + 4, :].bitcast(I32),
                in_=x_scales[0, 4 * q : 4 * q + 4, :].bitcast(I32),
            )

        zeros = sb.tile([P, P], F32, name="zeros", tag="late")
        ident = sb.tile([P, P], F32, name="ident")
        nc.gpsimd.memset(zeros[:], 0.0)
        nc.gpsimd.affine_select(
            out=ident[:], in_=zeros[:], compare_op=ALU.not_equal, fill=1.0, base=0, pattern=[[-1, P]], channel_multiplier=1
        )
        nc.gpsimd.memset(count_window[0:ROW, T // 2 : T], 0.0)

        late = sb.tile([P, PACK * V + BLOCKS * S], F32, name="late", tag="late")
        h_raw = late[:, 0 : PACK * V].rearrange("p (j c) -> p j c", j=PACK)
        labels = [late[:, PACK * V + b * S : PACK * V + (b + 1) * S] for b in range(BLOCKS)]
        nc.sync.dma_start(out=late[:, 0 : PACK * V], in_=hT.rearrange("(p j) c -> p (j c)", j=PACK))
        lab_rows = lab.rearrange("(p b) s -> p b s", b=BLOCKS)
        out_rows = out.rearrange("(p b) s -> p b s", b=BLOCKS)
        for b in range(BLOCKS):
            nc.sync.dma_start(out=labels[b], in_=lab_rows[:, b, :])

        one = sb.tile([P, 1], F32, name="one")
        nc.gpsimd.memset(one[:], 1.0)

        addends = sb.tile([P, LOGS, STEPS_PADDED], F32, name="addends")
        for i in range(DEG):
            nc.scalar.activation(out=addends[:, :, DEG - 1 - i], in_=one[:].to_broadcast([P, LOGS]), func=ACT.Copy, scale=SERIES[i])
        factors = [sb.tile([P, STEPS], F32, name="factors%d" % n) for n in range(LOGS)]
        for n in range(LOGS):
            nc.scalar.activation(out=factors[n][:, DEG:STEPS], in_=one[:], func=ACT.Copy, scale=LOG_GAINS[n])

        def scaled_log(n, total, shift):
            bits = total.bitcast(U32)
            inverse = sb.tile([P, 1], F32, name="inverse%d" % n)
            nc.scalar.activation(out=inverse[:], in_=bits, func=ACT.Exp, scale=-BITS_SCALE, bias=-BITS_BIAS)
            nc.scalar.activation(out=addends[:, n, DEG:STEPS], in_=bits, func=ACT.Identity, scale=LOG_GAINS[n] * BITS_SCALE, bias=shift)
            repeated = inverse[:].to_broadcast([P, DEG])
            if n == BLOCKS:
                nc.vector.tensor_scalar(out=factors[n][:, 0:DEG], in0=repeated, scalar1=total, scalar2=-1.0, op0=ALU.mult, op1=ALU.add)
            else:
                nc.scalar.activation(out=factors[n][:, 0:DEG], in_=repeated, func=ACT.Copy, scale=total, bias=-1.0)
            horner = sb.tile([P, STEPS], F32, name="horner%d" % n)
            nc.vector.tensor_tensor_scan(
                out=horner[:], data0=factors[n][:], data1=addends[:, n, 0:STEPS], initial=SERIES[DEG], op0=ALU.mult, op1=ALU.add
            )
            return horner[:, DEG:STEPS]

        counts = sb.tile([P, S], F32, name="counts")
        nc.vector.tensor_copy(out=counts[:], in_=count_window[:].indirect(offsets[:]))
        x_codes = [sb.tile([P, HALF], U32, name="x_codes%d" % h, align_bytes=64) for h in range(2)]
        x_scale = [sb.tile([P, HALF], U8, name="x_scale%d" % h, align_bytes=64) for h in range(2)]
        for h in range(2):
            picked = offsets[:, h * HALF // LIST_ROWS : (h + 1) * HALF // LIST_ROWS]
            nc.vector.tensor_copy(out=x_codes[h][:], in_=word_window[:].bitcast(U32).indirect(picked))
            nc.vector.tensor_copy(out=x_scale[h][:], in_=scale_window[:].indirect(picked))

        own_rows = ps.tile([P, V], F32, name="own_rows")
        for b in range(BLOCKS):
            nc.tensor.transpose(own_rows[:, b * P : (b + 1) * P], own[:, b : b + 1].to_broadcast([P, P]), ident[:])
        counts_t = ps.tile([P, CHUNKS, P], F32, name="counts_t")
        for c in range(CHUNKS):
            nc.tensor.transpose(counts_t[:, c, :], counts[:, c * P : (c + 1) * P], ident[:])
        gap_col = sb.tile([P, CHUNKS], F32, name="gap_col")
        cap_col = sb.tile([P, CHUNKS], F32, name="cap_col")
        nc.scalar.activation(out=gap_col[:], in_=counts_t[:, :, ROW], func=ACT.Copy, scale=-(0.5 - 0.05) / KINK)
        nc.scalar.activation(out=cap_col[:], in_=counts_t[:, :, ROW], func=ACT.Copy, scale=-0.05 / KINK)
        neg_mit = [ps.tile([P, S], F32, name="neg_mit%d" % b) for b in range(BLOCKS)]
        for b in range(BLOCKS):
            for c in range(CHUNKS):
                nc.tensor.matmul(
                    neg_mit[b][:, c * P : (c + 1) * P],
                    lhsT=cap_col[:, c : c + 1].to_broadcast([P, P]),
                    rhs=ident[:],
                    is_transpose=True,
                    start=(c == 0),
                    stop=False,
                )

        def add_shortfall(b, tag):
            short_t = sb.tile([P, S], F32, name="short_t%d" % b, tag=tag, align_bytes=64)
            for c in range(CHUNKS):
                cols = slice(c * P, (c + 1) * P)
                nc.scalar.activation(
                    out=short_t[:, cols], in_=own_rows[:, b * P : (b + 1) * P], func=ACT.Relu, scale=-1.0 / KINK, bias=gap_col[:, c : c + 1]
                )
                nc.tensor.matmul(neg_mit[b][:, cols], lhsT=short_t[:, cols], rhs=ident[:], is_transpose=True, start=False, stop=(c == CHUNKS - 1))

        add_shortfall(0, "short_t0")

        grouped = [sb.tile([P, P, PACK], BF16, name="grouped%d" % b, tag="grouped%d" % b, align_bytes=64) for b in range(BLOCKS)]
        z = []
        for b in range(BLOCKS):
            nc.scalar.copy(out=grouped[b][:], in_=h_raw[:, :, b:V:BLOCKS].rearrange("p j c -> p c j"))
            h_codes = sb.tile([P, P], U32, name="h_codes%d" % b, align_bytes=64)
            h_scale = sb.tile([P, P], U8, name="h_scale%d" % b, align_bytes=64)
            nc.vector.quantize_mx(out=h_codes[:].bitcast(FP8X4), scales=h_scale[:], in_=grouped[b][:].rearrange("p c j -> p (c j)"))
            product = ps.tile([P, S], F32, name="z%d" % b)
            for h in range(2):
                nc.tensor.matmul_mx(
                    out=product[:, h * HALF : (h + 1) * HALF],
                    lhsT=h_codes[:].bitcast(FP8X4),
                    lhsT_scale=h_scale[:],
                    rhs=x_codes[h][:].bitcast(FP8X4),
                    rhs_scale=x_scale[h][:],
                    start=True,
                    stop=True,
                )
            z.append(product)
        add_shortfall(1, "grouped1")

        def wide(name, b):
            return sb.tile([P, S], F32, name="%s%d" % (name, b))

        def column(name, b):
            return sb.tile([P, 1], F32, name="%s%d" % (name, b))

        masked = [wide("masked", b) for b in range(BLOCKS)]
        ex = [wide("ex", b) for b in range(BLOCKS)]
        lifted = [wide("lifted", b) for b in range(BLOCKS)]
        base = [wide("base", b) for b in range(BLOCKS)]
        raised = [wide("raised", b) for b in range(BLOCKS)]
        result = [wide("result", b) for b in range(BLOCKS)]
        neg_max = [column("neg_max", b) for b in range(BLOCKS)]
        denom = [column("denom", b) for b in range(BLOCKS)]
        tz = [column("tz", b) for b in range(BLOCKS)]
        exp_shift = [column("exp_shift", b) for b in range(BLOCKS)]
        second_shift = [sb.tile([P, 1], F32, name="second_shift%d" % b, tag="second_shift%d" % b) for b in range(BLOCKS)]
        first_shift = [column("first_shift", b) for b in range(BLOCKS)]

        def mask(b):
            nc.vector.scalar_tensor_tensor(out=masked[b][:], in0=labels[b], scalar=1.0, in1=neg_mit[b][:], op0=ALU.subtract, op1=ALU.mult)

        mask(0)
        neg_scaled = sb.tile([P, S], F32, name="neg_scaled")
        peak = [column("peak", b) for b in range(BLOCKS)]
        to_neg_max = [KINK, -GAIN]
        knee = []
        for b in range(BLOCKS):
            if b == 0:
                nc.vector.tensor_scalar(
                    out=neg_scaled[:], in0=z[b][:], scalar1=-GAIN / KINK, scalar2=None, op0=ALU.mult, op1=ALU.min, accum_out=peak[b][:]
                )
                nc.gpsimd.tensor_tensor(out=base[b][:], in0=masked[b][:], in1=neg_scaled[:], op=ALU.subtract)
            else:
                nc.vector.tensor_reduce(out=peak[b][:], in_=z[b][:], axis=mybir.AxisListType.X, op=ALU.max)
            nc.vector.scalar_tensor_tensor(out=lifted[b][:], in0=labels[b], scalar=LIFT / GAIN, in1=z[b][:], op0=ALU.mult, op1=ALU.add)
            nc.scalar.activation(out=neg_max[b][:], in_=peak[b][:], func=ACT.Copy, scale=to_neg_max[b])
            nc.scalar.activation(
                out=first_shift[b][:], in_=peak[b][:], func=ACT.Copy, scale=-to_neg_max[b] / GAIN, bias=(BITS_BIAS + math.log(FLOOR)) / GAIN
            )
            nc.scalar.activation(out=second_shift[b][:], in_=peak[b][:], func=ACT.Copy, scale=BOTH * to_neg_max[b], bias=-BITS_BIAS)
            nc.scalar.activation(out=exp_shift[b][:], in_=peak[b][:], func=ACT.Copy, scale=BOTH * to_neg_max[b])
            nc.scalar.activation(out=ex[b][:], in_=lifted[b][:], func=ACT.Exp, scale=GAIN, bias=neg_max[b][:], accum_out=denom[b][:])
            knee.append(scaled_log(b, denom[b][:], first_shift[b][:]))
        mask(1)
        nc.vector.scalar_tensor_tensor(out=base[1][:], in0=z[1][:], scalar=GAIN / KINK, in1=masked[1][:], op0=ALU.mult, op1=ALU.add)

        ez_tags = ["ez0", "second_shift0"]
        for b in range(BLOCKS):
            nc.vector.scalar_tensor_tensor(out=raised[b][:], in0=z[b][:], scalar=knee[b], in1=base[b][:], op0=ALU.max, op1=ALU.add)
            ez = sb.tile([P, S], F32, name="ez%d" % b, tag=ez_tags[b])
            nc.scalar.activation(out=ez[:], in_=raised[b][:], func=ACT.Exp, scale=KINK, bias=exp_shift[b][:], accum_out=tz[b][:])
            level = scaled_log(BLOCKS + b, tz[b][:], second_shift[b][:])
            if b == 0:
                pieces = [(slice(0, S), nc.sync)]
            else:
                pieces = [(slice(0, HALF), nc.sync), (slice(HALF, S), nc.scalar)]
            for cols, queue in pieces:
                nc.vector.tensor_scalar(out=result[b][:, cols], in0=raised[b][:, cols], scalar1=KINK, scalar2=level, op0=ALU.mult, op1=ALU.add)
                queue.dma_start(out=out_rows[:, b, cols], in_=result[b][:, cols])
